import numpy as np
import ml_dtypes


def mxq(x, axis, fmt="e4m3"):
    dtype, down = {"e4m3": (ml_dtypes.float8_e4m3fn, 7), "e5m2": (ml_dtypes.float8_e5m2, 14)}[fmt]
    v = np.moveaxis(np.asarray(x, np.float32).astype(ml_dtypes.bfloat16).astype(np.float64), axis, -1)
    blocks = v.reshape(v.shape[:-1] + (-1, 32))
    amax = np.abs(blocks).max(-1, keepdims=True)
    byte = np.maximum(np.where(amax > 0, np.frexp(amax)[1] - 1 + 127, 0) - down, 1)
    scale = np.exp2(byte - 127.0)
    codes = (blocks / scale).astype(np.float32).astype(dtype).astype(np.float64)
    return np.moveaxis((codes * scale).reshape(v.shape), -1, axis)


WIDE = False


def mx_kscale(k):
    if not WIDE:
        return np.ones(k)
    levels = np.array([10, -10, 5, -5, 0])
    if k % 512:
        return np.exp2(np.random.permutation(np.resize(levels, k // 32))).repeat(32)
    a = np.empty((k // 512, 16))
    for p in range(k // 512):
        a[p, :8] = np.random.permutation(np.resize(levels, 8))
        for g in range(8):
            far = levels[np.abs(levels - a[p, g]) >= 10]
            a[p, g + 8] = far[np.random.randint(len(far))]
    return np.exp2(a.ravel()).repeat(32)


def f64(x):
    return np.asarray(x).astype(np.float64)


def striped(idx):
    return np.tile(idx.reshape(-1, 16).T, (8, 1)).astype(np.uint16)


def unstriped(offs):
    return offs[:16].T.reshape(-1).astype(np.int64)


def striped8(idx):
    return np.concatenate([x.reshape(-1, 16).T for x in idx]).astype(np.uint16)


def runs(offs, k):
    lists = np.stack([offs[16 * r : 16 * r + 16].T.reshape(-1) for r in range(8)]).astype(np.int64)
    return lists[np.arange(k) % 512 // 64]


def pack_weight(w):
    k, n = w.shape
    w = f64(np.asarray(w, np.float32).astype(ml_dtypes.bfloat16)).reshape(k // 32, 32, n)
    amax = np.abs(w).max(1)
    byte = np.clip(np.where(amax > 0, np.frexp(amax)[1] - 1 + 127 - 7, 1), 1, 254)
    scaled = (w * np.exp2(127.0 - byte)[:, None, :]).reshape(k, n).astype(np.float32)
    words = np.ascontiguousarray(scaled.reshape(k // 512, 128, 4, n).transpose(0, 1, 3, 2)).astype(ml_dtypes.float8_e4m3fn).view(np.uint8)
    return words, np.ascontiguousarray(byte.astype(np.uint8).reshape(k // 512, 16, n))


def unpack_weight(words, scales):
    g, p, n, _ = words.shape
    vals = np.ascontiguousarray(words).view(ml_dtypes.float8_e4m3fn).astype(np.float64) * np.repeat(np.exp2(scales.astype(np.float64) - 127.0), 8, axis=1)[..., None]
    return vals.transpose(0, 1, 3, 2).reshape(g * 512, n)


def relu(v):
    return np.maximum(v, 0.0)


def sigmoid(v):
    return 1.0 / (1.0 + np.exp(-np.maximum(v, -700.0)))


K, T, S, G, H, W = 512, 1024, 256, 2048, 512, 192


def setup_inputs():
    n = np.random.standard_normal
    s = mx_kscale(K)[:, None]
    packed_xT = pack_weight(n((K, T)) * s)
    packed_dT = pack_weight(n((K, G)) / s)
    return {
        "x_words": packed_xT[0],
        "x_scales": packed_xT[1],
        "d_words": packed_dT[0],
        "d_scales": packed_dT[1],
        "gs": (np.random.uniform(0.5, 1.5, (K, 1)) * s).astype(np.float32),
        "offs": striped(np.random.permutation(T)[:S]),
        "k1": striped8(np.random.randint(0, G, (8, H))),
        "n1": striped(np.random.permutation(S)[:W]),
        "n2": striped(np.random.permutation(S)[:W]),
        "k2": striped8(np.random.randint(0, G, (8, H))),
        "n3": striped8(np.stack([np.random.permutation(S) for _ in range(8)])),
        "n4": striped8(np.stack([np.random.permutation(S) for _ in range(8)])),
    }


def reference(x_words, x_scales, d_words, d_scales, gs, offs, k1, n1, n2, k2, n3, n4):
    d_k2 = unpack_weight(d_words, d_scales)[np.arange(K)[:, None], runs(k2, K)]
    d_k1 = unpack_weight(d_words, d_scales)[np.arange(K)[:, None], runs(k1, K)]
    xq = unpack_weight(x_words, x_scales)[:, unstriped(offs)]
    h = 0.0625 * (d_k1.T @ xq)
    old = h[:, unstriped(n1)]
    pa = h[:, unstriped(n2)]
    ra = old * sigmoid(pa)
    ds = h.copy()
    ds[:, unstriped(n1)] = ra
    z = f64(gs) * ds
    h2 = 0.0625 * ((d_k2.T @ mxq(z, 0, "e4m3")))
    return relu(h2 - (h2[np.arange(H)[:, None], runs(n3, H)])) + 0.5 * (relu(h2[np.arange(H)[:, None], runs(n4, H)] - h2))

@@ -1,0 +1,160 @@
+from contextlib import ExitStack
+
+import concourse.mybir as mybir
+
+K, T, S, G, H, W = 512, 1024, 256, 2048, 512, 192
+FLOPS = 2 * 2 * K * H * S
+
+F32 = mybir.dt.float32
+BF16 = mybir.dt.bfloat16
+I32 = mybir.dt.int32
+U32 = mybir.dt.uint32
+U16 = mybir.dt.uint16
+U8 = mybir.dt.uint8
+FP8X4 = mybir.dt.float8_e4m3fn_x4
+ALU = mybir.AluOpType
+ACT = mybir.ActivationFunctionType
+
+P = 128
+PACK = 4
+WINDOW = 2 * S
+
+
+def tile_picked_codekgatehinge_none_p_kernel(
+    tc, x_words, x_scales, d_words, d_scales, gs, offs, k1, n1, n2, k2, n3, n4, out
+):
+    nc = tc.nc
+    with ExitStack() as ctx:
+        lists = ctx.enter_context(tc.tile_pool(name="lists", bufs=1))
+        keep = ctx.enter_context(tc.tile_pool(name="keep", bufs=1))
+        psum = ctx.enter_context(tc.psum_pool(name="psum", bufs=1))
+
+        def load_list(src, name):
+            tile = lists.tile(list(src.shape), U16, name=name)
+            nc.sync.dma_start(tile[:], src)
+            return tile
+
+        def sbuf(shape, dtype, name, tag=""):
+            return keep.tile(shape, dtype, name=name, tag=tag or name, align_bytes=64)
+
+        d_scale_table = sbuf([P, G], U8, "d_scale_table")
+        x_scale_table = sbuf([P, T], U8, "x_scale_table", "x_side")
+        d_word_table = sbuf([P, G], U32, "d_word_table")
+        x_word_table = sbuf([P, T], U32, "x_word_table")
+        nc.vector.memset(d_scale_table[:].bitcast(I32), 0)
+        nc.vector.memset(x_scale_table[:].bitcast(I32), 0)
+
+        k1_list = load_list(k1, "k1_list")
+        offs_list = load_list(offs, "offs_list")
+        for r in range(2):
+            nc.scalar.dma_start(d_scale_table[r:P:16, :].bitcast(I32), d_scales[0, r:16:2, :].bitcast(I32))
+        for r in range(2):
+            nc.scalar.dma_start(x_scale_table[r:P:16, :].bitcast(I32), x_scales[0, r:16:2, :].bitcast(I32))
+        n2_list = load_list(n2, "n2_list")
+        n1_list = load_list(n1, "n1_list")
+        k2_list = load_list(k2, "k2_list")
+        n4_list = load_list(n4, "n4_list")
+        n3_list = load_list(n3, "n3_list")
+        nc.sync.dma_start(d_word_table[:].bitcast(I32), d_words[0].rearrange("p n t -> p (n t)").bitcast(I32))
+        nc.sync.dma_start(x_word_table[:].bitcast(I32), x_words[0].rearrange("p n t -> p (n t)").bitcast(I32))
+
+        windows = [sbuf([P, WINDOW], F32, f"window{t}") for t in range(PACK)]
+        for t in range(PACK):
+            nc.vector.memset(windows[t][:, S:], 0.0)
+
+        def deal(dst, src):
+            nc.vector.tensor_copy(
+                dst.rearrange("p (t m) -> p t m", t=PACK), src.rearrange("p (m t) -> p t m", t=PACK)
+            )
+
+        def pick(table, a_list, dtype, name, tag, pieces=1):
+            n = a_list.shape[1] * 16
+            picked = sbuf([P, n], dtype, name, tag)
+            cols = n // pieces
+            for i in range(pieces):
+                nc.vector.tensor_copy(
+                    picked[:, i * cols : (i + 1) * cols],
+                    table[:].indirect(a_list[:, i * cols // 16 : (i + 1) * cols // 16]),
+                )
+            return picked
+
+        def place_odd_runs(plane, queue):
+            for r in range(2):
+                queue.dma_start(plane[2 + r : P : 32, :].bitcast(I32), plane[16 + r : P : 32, :].bitcast(I32))
+
+        s1_picked = pick(d_scale_table, k1_list, U8, "s1_picked", "k1_side")
+        xs_picked = pick(x_scale_table, offs_list, U8, "xs_picked", "xs_picked")
+        scales1 = sbuf([P, H + S], U8, "scales1")
+        deal(scales1[:, :H], s1_picked[:])
+        nc.vector.tensor_copy(scales1[:, H:].bitcast(I32), xs_picked[:].bitcast(I32))
+        place_odd_runs(scales1, nc.scalar)
+        w1_scales = scales1[:, :H]
+        x_sc = scales1[:, H:]
+        gain = sbuf([P, PACK], F32, "gain", "xs_picked")
+        nc.sync.dma_start(gain[:], gs.rearrange("(p t) o -> p (t o)", t=PACK))
+        w1_picked = pick(d_word_table, k1_list, U32, "w1_picked", "k1_side")
+        x_w = pick(x_word_table, offs_list, U32, "x_w", "x_side")
+        w1_words = sbuf([P, H], U32, "w1_words")
+        deal(w1_words[:], w1_picked[:])
+
+        def product(t, words, scales, rhs_words, rhs_scales, name):
+            bank = psum.tile([P, S], F32, name=f"{name}{t}")
+            cols = slice(t * P, (t + 1) * P)
+            nc.tensor.matmul_mx(
+                out=bank[:],
+                lhsT=words[:, cols].bitcast(FP8X4),
+                lhsT_scale=scales[:, cols],
+                rhs=rhs_words[:].bitcast(FP8X4),
+                rhs_scale=rhs_scales,
+                start=True,
+                stop=True,
+            )
+            nc.vector.tensor_scalar(windows[t][:, :S], bank[:], 0.0625, None, ALU.mult)
+
+        z = keep.tile([P, S, PACK], BF16, name="z", align_bytes=64)
+        gated = [keep.tile([P, W], F32, name=f"gated{t}", align_bytes=64) for t in range(PACK)]
+
+        def fetch1(t):
+            gate = keep.tile([P, W], F32, name=f"gate{t}", align_bytes=64)
+            old = sbuf([P, W], F32, f"old{t}")
+            nc.scalar.activation(gate[:], windows[t][:].indirect(n2_list[:]), ACT.Sigmoid)
+            nc.scalar.activation(old[:], windows[t][:].indirect(n1_list[:]), ACT.Copy)
+            nc.vector.tensor_tensor(gated[t][:], old[:], gate[:], ALU.mult)
+
+        def put1(t):
+            nc.scalar.activation(windows[t][:].indirect(n1_list[:]), gated[t][:], ACT.Copy)
+            nc.vector.tensor_scalar(z[:, :, t], windows[t][:, :S], gain[:, t : t + 1], None, ALU.mult)
+
+        for t in range(PACK):
+            product(t, w1_words, w1_scales, x_w, x_sc, "h1_")
+        s2_picked = pick(d_scale_table, k2_list, U8, "s2_picked", "x_side", 2)
+        w2_scales = sbuf([P, H], U8, "w2_scales")
+        deal(w2_scales[:], s2_picked[:])
+        place_odd_runs(w2_scales, nc.sync)
+        for t in range(PACK):
+            fetch1(t)
+        w2_picked = pick(d_word_table, k2_list, U32, "w2_picked", "old0", 2)
+        w2_words = sbuf([P, H], U32, "w2_words")
+        deal(w2_words[:], w2_picked[:])
+        for t in range(PACK):
+            put1(t)
+
+        z_words = keep.tile([P, S], U32, name="z_words", align_bytes=64)
+        z_scales = keep.tile([P, S], U8, name="z_scales", align_bytes=64)
+        nc.vector.quantize_mx(out=z_words[:].bitcast(FP8X4), scales=z_scales[:], in_=z[:].rearrange("p s t -> p (s t)"))
+
+        for t in range(PACK):
+            product(t, w2_words, w2_scales, z_words, z_scales[:], "h2_")
+        out_rows = out.rearrange("(p t) s -> t p s", t=PACK)
+        for t in range(PACK):
+            h2 = windows[t][:, :S]
+            above = keep.tile([P, S], F32, name=f"above{t}", align_bytes=64)
+            below = keep.tile([P, S], F32, name=f"below{t}", align_bytes=64)
+            res = keep.tile([P, S], F32, name=f"res{t}", align_bytes=64)
+            nc.scalar.activation(above[:], windows[t][:].indirect(n4_list[:]), ACT.Copy)
+            nc.scalar.activation(below[:], windows[t][:].indirect(n3_list[:]), ACT.Copy)
+            nc.vector.tensor_tensor(above[:], above[:], h2, ALU.subtract)
+            nc.vector.tensor_scalar(above[:], above[:], 0.0, 0.5, ALU.max, ALU.mult)
+            nc.vector.tensor_tensor(below[:], h2, below[:], ALU.subtract)
+            nc.vector.scalar_tensor_tensor(res[:], below[:], 0.0, above[:], ALU.max, ALU.add)
+            nc.sync.dma_start(out_rows[t], res[:])

@@ -42,21 +42,19 @@ def tile_picked_codekgatehinge_none_p_kernel(
         d_word_table = sbuf([P, G], U32, "d_word_table")
         x_word_table = sbuf([P, T], U32, "x_word_table")
         nc.vector.memset(d_scale_table[:].bitcast(I32), 0)
-        nc.vector.memset(x_scale_table[:].bitcast(I32), 0)
+        nc.gpsimd.memset(x_scale_table[:].bitcast(I32), 0)
 
-        k1_list = load_list(k1, "k1_list")
         offs_list = load_list(offs, "offs_list")
-        for r in range(2):
-            nc.scalar.dma_start(d_scale_table[r:P:16, :].bitcast(I32), d_scales[0, r:16:2, :].bitcast(I32))
-        for r in range(2):
-            nc.scalar.dma_start(x_scale_table[r:P:16, :].bitcast(I32), x_scales[0, r:16:2, :].bitcast(I32))
+        k1_list = load_list(k1, "k1_list")
+        nc.sync.dma_start(x_scale_table[0:P:8, :].bitcast(I32), x_scales[0].bitcast(I32))
+        nc.sync.dma_start(d_scale_table[0:P:8, :].bitcast(I32), d_scales[0].bitcast(I32))
         n2_list = load_list(n2, "n2_list")
         n1_list = load_list(n1, "n1_list")
         k2_list = load_list(k2, "k2_list")
-        n4_list = load_list(n4, "n4_list")
-        n3_list = load_list(n3, "n3_list")
         nc.sync.dma_start(d_word_table[:].bitcast(I32), d_words[0].rearrange("p n t -> p (n t)").bitcast(I32))
         nc.sync.dma_start(x_word_table[:].bitcast(I32), x_words[0].rearrange("p n t -> p (n t)").bitcast(I32))
+        n4_list = load_list(n4, "n4_list")
+        n3_list = load_list(n3, "n3_list")
 
         windows = [sbuf([P, WINDOW], F32, f"window{t}") for t in range(PACK)]
         for t in range(PACK):
@@ -65,6 +63,12 @@ def tile_picked_codekgatehinge_none_p_kernel(
         def deal(dst, src):
             nc.vector.tensor_copy(
                 dst.rearrange("p (t m) -> p t m", t=PACK), src.rearrange("p (m t) -> p t m", t=PACK)
+            )
+
+        def deal_tiles(dst, src, t0, t1):
+            nc.vector.tensor_copy(
+                dst.rearrange("p (t m) -> p t m", t=PACK)[:, t0:t1, :],
+                src.rearrange("p (m t) -> p t m", t=PACK)[:, t0:t1, :],
             )
 
         def pick(table, a_list, dtype, name, tag, pieces=1):
@@ -78,38 +82,42 @@ def tile_picked_codekgatehinge_none_p_kernel(
                 )
             return picked
 
-        def place_odd_runs(plane, queue):
-            for r in range(2):
-                queue.dma_start(plane[2 + r : P : 32, :].bitcast(I32), plane[16 + r : P : 32, :].bitcast(I32))
-
-        s1_picked = pick(d_scale_table, k1_list, U8, "s1_picked", "k1_side")
         xs_picked = pick(x_scale_table, offs_list, U8, "xs_picked", "xs_picked")
+        s1_picked = pick(d_scale_table, k1_list, U8, "s1_picked", "k1_side")
         scales1 = sbuf([P, H + S], U8, "scales1")
-        deal(scales1[:, :H], s1_picked[:])
         nc.vector.tensor_copy(scales1[:, H:].bitcast(I32), xs_picked[:].bitcast(I32))
-        place_odd_runs(scales1, nc.scalar)
+        deal(scales1[:, :H], s1_picked[:])
+        for r in range(1, 4):
+            queue = nc.sync if r % 2 else nc.scalar
+            queue.dma_start(scales1[r:P:32, :].bitcast(I32), scales1[8 * r : P : 32, :].bitcast(I32))
         w1_scales = scales1[:, :H]
         x_sc = scales1[:, H:]
-        gain = sbuf([P, PACK], F32, "gain", "xs_picked")
-        nc.sync.dma_start(gain[:], gs.rearrange("(p t) o -> p (t o)", t=PACK))
-        w1_picked = pick(d_word_table, k1_list, U32, "w1_picked", "k1_side")
+        w1_picked = pick(d_word_table, k1_list, U32, "w1_picked", "w1_picked")
+        w1_first = sbuf([P, P], U32, "w1_first")
         x_w = pick(x_word_table, offs_list, U32, "x_w", "x_side")
-        w1_words = sbuf([P, H], U32, "w1_words")
-        deal(w1_words[:], w1_picked[:])
+        nc.vector.tensor_copy(w1_first[:], w1_picked[:, 0:H:PACK])
+        w1_rest = sbuf([P, H - P], U32, "w1_rest", "x_word_table")
+        gain = sbuf([P, PACK], F32, "gain", "k1_side")
+        nc.sync.dma_start(gain[:], gs.rearrange("(p t) o -> p (t o)", t=PACK))
 
-        def product(t, words, scales, rhs_words, rhs_scales, name):
-            bank = psum.tile([P, S], F32, name=f"{name}{t}")
-            cols = slice(t * P, (t + 1) * P)
+        def product(t, words, scales, rhs_words, rhs_scales, cols, tag, on_scalar):
+            bank = psum.tile([P, cols.stop - cols.start], F32, name=tag, tag=tag)
+            rows = slice(t * P, (t + 1) * P)
             nc.tensor.matmul_mx(
                 out=bank[:],
-                lhsT=words[:, cols].bitcast(FP8X4),
-                lhsT_scale=scales[:, cols],
-                rhs=rhs_words[:].bitcast(FP8X4),
-                rhs_scale=rhs_scales,
+                lhsT=words.bitcast(FP8X4),
+                lhsT_scale=scales[:, rows],
+                rhs=rhs_words[:, cols].bitcast(FP8X4),
+                rhs_scale=rhs_scales[:, cols],
                 start=True,
                 stop=True,
             )
-            nc.vector.tensor_scalar(windows[t][:, :S], bank[:], 0.0625, None, ALU.mult)
+            if on_scalar:
+                nc.scalar.activation(windows[t][:, cols], bank[:], ACT.Copy, scale=0.0625)
+            else:
+                nc.vector.tensor_scalar(windows[t][:, cols], bank[:], 0.0625, None, ALU.mult)
+
+        halves = (slice(0, S // 2), slice(S // 2, S))
 
         z = keep.tile([P, S, PACK], BF16, name="z", align_bytes=64)
         gated = [keep.tile([P, W], F32, name=f"gated{t}", align_bytes=64) for t in range(PACK)]
@@ -123,14 +131,20 @@ def tile_picked_codekgatehinge_none_p_kernel(
 
         def put1(t):
             nc.scalar.activation(windows[t][:].indirect(n1_list[:]), gated[t][:], ACT.Copy)
-            nc.vector.tensor_scalar(z[:, :, t], windows[t][:, :S], gain[:, t : t + 1], None, ALU.mult)
+            for cols in halves if t == PACK - 1 else (slice(0, S),):
+                nc.vector.tensor_scalar(z[:, cols, t], windows[t][:, cols], gain[:, t : t + 1], None, ALU.mult)
 
-        for t in range(PACK):
-            product(t, w1_words, w1_scales, x_w, x_sc, "h1_")
+        for i, cols in enumerate(halves):
+            product(0, w1_first[:], w1_scales, x_w, x_sc, cols, f"half{i}", False)
+        for t in range(1, PACK):
+            w1_t = w1_rest[:, (t - 1) * P : t * P]
+            nc.vector.tensor_copy(w1_t, w1_picked[:, t:H:PACK])
+            product(t, w1_t, w1_scales, x_w, x_sc, slice(0, S), f"bank{t}", False)
         s2_picked = pick(d_scale_table, k2_list, U8, "s2_picked", "x_side", 2)
         w2_scales = sbuf([P, H], U8, "w2_scales")
         deal(w2_scales[:], s2_picked[:])
-        place_odd_runs(w2_scales, nc.sync)
+        for r in range(1, 4):
+            nc.sync.dma_start(w2_scales[r:P:32, :].bitcast(I32), w2_scales[8 * r : P : 32, :].bitcast(I32))
         for t in range(PACK):
             fetch1(t)
         w2_picked = pick(d_word_table, k2_list, U32, "w2_picked", "old0", 2)
@@ -141,20 +155,28 @@ def tile_picked_codekgatehinge_none_p_kernel(
 
         z_words = keep.tile([P, S], U32, name="z_words", align_bytes=64)
         z_scales = keep.tile([P, S], U8, name="z_scales", align_bytes=64)
-        nc.vector.quantize_mx(out=z_words[:].bitcast(FP8X4), scales=z_scales[:], in_=z[:].rearrange("p s t -> p (s t)"))
+        for cols in halves:
+            nc.vector.quantize_mx(
+                out=z_words[:, cols].bitcast(FP8X4),
+                scales=z_scales[:, cols],
+                in_=z[:, cols, :].rearrange("p s t -> p (s t)"),
+            )
 
-        for t in range(PACK):
-            product(t, w2_words, w2_scales, z_words, z_scales[:], "h2_")
+        for i, cols in enumerate(halves):
+            product(0, w2_words[:, :P], w2_scales, z_words, z_scales, cols, f"half{i}", True)
+        for t in range(1, PACK):
+            product(t, w2_words[:, t * P : (t + 1) * P], w2_scales, z_words, z_scales, slice(0, S), f"bank{t}", False)
         out_rows = out.rearrange("(p t) s -> t p s", t=PACK)
         for t in range(PACK):
-            h2 = windows[t][:, :S]
-            above = keep.tile([P, S], F32, name=f"above{t}", align_bytes=64)
-            below = keep.tile([P, S], F32, name=f"below{t}", align_bytes=64)
-            res = keep.tile([P, S], F32, name=f"res{t}", align_bytes=64)
+            above = sbuf([P, S], F32, f"above{t}")
+            below = sbuf([P, S], F32, f"below{t}")
+            res = sbuf([P, S], F32, f"res{t}")
             nc.scalar.activation(above[:], windows[t][:].indirect(n4_list[:]), ACT.Copy)
-            nc.scalar.activation(below[:], windows[t][:].indirect(n3_list[:]), ACT.Copy)
-            nc.vector.tensor_tensor(above[:], above[:], h2, ALU.subtract)
+            nc.vector.tensor_tensor(above[:], above[:], windows[t][:, :S], ALU.subtract)
             nc.vector.tensor_scalar(above[:], above[:], 0.0, 0.5, ALU.max, ALU.mult)
-            nc.vector.tensor_tensor(below[:], h2, below[:], ALU.subtract)
-            nc.vector.scalar_tensor_tensor(res[:], below[:], 0.0, above[:], ALU.max, ALU.add)
-            nc.sync.dma_start(out_rows[t], res[:])
+            for cols in halves if t == PACK - 1 else (slice(0, S),):
+                offsets = n3_list[:, cols.start // 16 : cols.stop // 16]
+                nc.scalar.activation(below[:, cols], windows[t][:].indirect(offsets), ACT.Copy)
+                nc.vector.tensor_tensor(below[:, cols], windows[t][:, cols], below[:, cols], ALU.subtract)
+                nc.vector.scalar_tensor_tensor(res[:, cols], below[:, cols], 0.0, above[:, cols], ALU.max, ALU.add)
+                nc.sync.dma_start(out_rows[t][:, cols], res[:, cols])

@@ -41,8 +41,8 @@ def tile_picked_codekgatehinge_none_p_kernel(
         x_scale_table = sbuf([P, T], U8, "x_scale_table", "x_side")
         d_word_table = sbuf([P, G], U32, "d_word_table")
         x_word_table = sbuf([P, T], U32, "x_word_table")
+        nc.vector.memset(x_scale_table[:].bitcast(I32), 0)
         nc.vector.memset(d_scale_table[:].bitcast(I32), 0)
-        nc.gpsimd.memset(x_scale_table[:].bitcast(I32), 0)
 
         offs_list = load_list(offs, "offs_list")
         k1_list = load_list(k1, "k1_list")
@@ -50,9 +50,9 @@ def tile_picked_codekgatehinge_none_p_kernel(
         nc.sync.dma_start(d_scale_table[0:P:8, :].bitcast(I32), d_scales[0].bitcast(I32))
         n2_list = load_list(n2, "n2_list")
         n1_list = load_list(n1, "n1_list")
-        k2_list = load_list(k2, "k2_list")
         nc.sync.dma_start(d_word_table[:].bitcast(I32), d_words[0].rearrange("p n t -> p (n t)").bitcast(I32))
         nc.sync.dma_start(x_word_table[:].bitcast(I32), x_words[0].rearrange("p n t -> p (n t)").bitcast(I32))
+        k2_list = load_list(k2, "k2_list")
         n4_list = load_list(n4, "n4_list")
         n3_list = load_list(n3, "n3_list")
 

from contextlib import ExitStack

import concourse.mybir as mybir

K, T, S, G, H, W = 512, 1024, 256, 2048, 512, 192
FLOPS = 2 * 2 * K * H * S

F32 = mybir.dt.float32
BF16 = mybir.dt.bfloat16
I32 = mybir.dt.int32
U32 = mybir.dt.uint32
U16 = mybir.dt.uint16
U8 = mybir.dt.uint8
FP8X4 = mybir.dt.float8_e4m3fn_x4
ALU = mybir.AluOpType
ACT = mybir.ActivationFunctionType

P = 128
PACK = 4
WINDOW = 2 * S


def tile_picked_codekgatehinge_none_p_kernel(
    tc, x_words, x_scales, d_words, d_scales, gs, offs, k1, n1, n2, k2, n3, n4, out
):
    nc = tc.nc
    with ExitStack() as ctx:
        lists = ctx.enter_context(tc.tile_pool(name="lists", bufs=1))
        keep = ctx.enter_context(tc.tile_pool(name="keep", bufs=1))
        psum = ctx.enter_context(tc.psum_pool(name="psum", bufs=1))

        def load_list(src, name):
            tile = lists.tile(list(src.shape), U16, name=name)
            nc.sync.dma_start(tile[:], src)
            return tile

        def sbuf(shape, dtype, name, tag=""):
            return keep.tile(shape, dtype, name=name, tag=tag or name, align_bytes=64)

        d_scale_table = sbuf([P, G], U8, "d_scale_table")
        x_scale_table = sbuf([P, T], U8, "x_scale_table", "x_side")
        d_word_table = sbuf([P, G], U32, "d_word_table")
        x_word_table = sbuf([P, T], U32, "x_word_table")
        nc.vector.memset(x_scale_table[:].bitcast(I32), 0)
        nc.vector.memset(d_scale_table[:].bitcast(I32), 0)

        offs_list = load_list(offs, "offs_list")
        k1_list = load_list(k1, "k1_list")
        nc.sync.dma_start(x_scale_table[0:P:8, :].bitcast(I32), x_scales[0].bitcast(I32))
        nc.sync.dma_start(d_scale_table[0:P:8, :].bitcast(I32), d_scales[0].bitcast(I32))
        n2_list = load_list(n2, "n2_list")
        n1_list = load_list(n1, "n1_list")
        nc.sync.dma_start(d_word_table[:].bitcast(I32), d_words[0].rearrange("p n t -> p (n t)").bitcast(I32))
        nc.sync.dma_start(x_word_table[:].bitcast(I32), x_words[0].rearrange("p n t -> p (n t)").bitcast(I32))
        k2_list = load_list(k2, "k2_list")
        n4_list = load_list(n4, "n4_list")
        n3_list = load_list(n3, "n3_list")

        windows = [sbuf([P, WINDOW], F32, f"window{t}") for t in range(PACK)]
        for t in range(PACK):
            nc.vector.memset(windows[t][:, S:], 0.0)

        def deal(dst, src):
            nc.vector.tensor_copy(
                dst.rearrange("p (t m) -> p t m", t=PACK), src.rearrange("p (m t) -> p t m", t=PACK)
            )

        def deal_tiles(dst, src, t0, t1):
            nc.vector.tensor_copy(
                dst.rearrange("p (t m) -> p t m", t=PACK)[:, t0:t1, :],
                src.rearrange("p (m t) -> p t m", t=PACK)[:, t0:t1, :],
            )

        def pick(table, a_list, dtype, name, tag, pieces=1):
            n = a_list.shape[1] * 16
            picked = sbuf([P, n], dtype, name, tag)
            cols = n // pieces
            for i in range(pieces):
                nc.vector.tensor_copy(
                    picked[:, i * cols : (i + 1) * cols],
                    table[:].indirect(a_list[:, i * cols // 16 : (i + 1) * cols // 16]),
                )
            return picked

        xs_picked = pick(x_scale_table, offs_list, U8, "xs_picked", "xs_picked")
        s1_picked = pick(d_scale_table, k1_list, U8, "s1_picked", "k1_side")
        scales1 = sbuf([P, H + S], U8, "scales1")
        nc.vector.tensor_copy(scales1[:, H:].bitcast(I32), xs_picked[:].bitcast(I32))
        deal(scales1[:, :H], s1_picked[:])
        for r in range(1, 4):
            queue = nc.sync if r % 2 else nc.scalar
            queue.dma_start(scales1[r:P:32, :].bitcast(I32), scales1[8 * r : P : 32, :].bitcast(I32))
        w1_scales = scales1[:, :H]
        x_sc = scales1[:, H:]
        w1_picked = pick(d_word_table, k1_list, U32, "w1_picked", "w1_picked")
        w1_first = sbuf([P, P], U32, "w1_first")
        x_w = pick(x_word_table, offs_list, U32, "x_w", "x_side")
        nc.vector.tensor_copy(w1_first[:], w1_picked[:, 0:H:PACK])
        w1_rest = sbuf([P, H - P], U32, "w1_rest", "x_word_table")
        gain = sbuf([P, PACK], F32, "gain", "k1_side")
        nc.sync.dma_start(gain[:], gs.rearrange("(p t) o -> p (t o)", t=PACK))

        def product(t, words, scales, rhs_words, rhs_scales, cols, tag, on_scalar):
            bank = psum.tile([P, cols.stop - cols.start], F32, name=tag, tag=tag)
            rows = slice(t * P, (t + 1) * P)
            nc.tensor.matmul_mx(
                out=bank[:],
                lhsT=words.bitcast(FP8X4),
                lhsT_scale=scales[:, rows],
                rhs=rhs_words[:, cols].bitcast(FP8X4),
                rhs_scale=rhs_scales[:, cols],
                start=True,
                stop=True,
            )
            if on_scalar:
                nc.scalar.activation(windows[t][:, cols], bank[:], ACT.Copy, scale=0.0625)
            else:
                nc.vector.tensor_scalar(windows[t][:, cols], bank[:], 0.0625, None, ALU.mult)

        halves = (slice(0, S // 2), slice(S // 2, S))

        z = keep.tile([P, S, PACK], BF16, name="z", align_bytes=64)
        gated = [keep.tile([P, W], F32, name=f"gated{t}", align_bytes=64) for t in range(PACK)]

        def fetch1(t):
            gate = keep.tile([P, W], F32, name=f"gate{t}", align_bytes=64)
            old = sbuf([P, W], F32, f"old{t}")
            nc.scalar.activation(gate[:], windows[t][:].indirect(n2_list[:]), ACT.Sigmoid)
            nc.scalar.activation(old[:], windows[t][:].indirect(n1_list[:]), ACT.Copy)
            nc.vector.tensor_tensor(gated[t][:], old[:], gate[:], ALU.mult)

        def put1(t):
            nc.scalar.activation(windows[t][:].indirect(n1_list[:]), gated[t][:], ACT.Copy)
            for cols in halves if t == PACK - 1 else (slice(0, S),):
                nc.vector.tensor_scalar(z[:, cols, t], windows[t][:, cols], gain[:, t : t + 1], None, ALU.mult)

        for i, cols in enumerate(halves):
            product(0, w1_first[:], w1_scales, x_w, x_sc, cols, f"half{i}", False)
        for t in range(1, PACK):
            w1_t = w1_rest[:, (t - 1) * P : t * P]
            nc.vector.tensor_copy(w1_t, w1_picked[:, t:H:PACK])
            product(t, w1_t, w1_scales, x_w, x_sc, slice(0, S), f"bank{t}", False)
        s2_picked = pick(d_scale_table, k2_list, U8, "s2_picked", "x_side", 2)
        w2_scales = sbuf([P, H], U8, "w2_scales")
        deal(w2_scales[:], s2_picked[:])
        for r in range(1, 4):
            nc.sync.dma_start(w2_scales[r:P:32, :].bitcast(I32), w2_scales[8 * r : P : 32, :].bitcast(I32))
        for t in range(PACK):
            fetch1(t)
        w2_picked = pick(d_word_table, k2_list, U32, "w2_picked", "old0", 2)
        w2_words = sbuf([P, H], U32, "w2_words")
        deal(w2_words[:], w2_picked[:])
        for t in range(PACK):
            put1(t)

        z_words = keep.tile([P, S], U32, name="z_words", align_bytes=64)
        z_scales = keep.tile([P, S], U8, name="z_scales", align_bytes=64)
        for cols in halves:
            nc.vector.quantize_mx(
                out=z_words[:, cols].bitcast(FP8X4),
                scales=z_scales[:, cols],
                in_=z[:, cols, :].rearrange("p s t -> p (s t)"),
            )

        for i, cols in enumerate(halves):
            product(0, w2_words[:, :P], w2_scales, z_words, z_scales, cols, f"half{i}", True)
        for t in range(1, PACK):
            product(t, w2_words[:, t * P : (t + 1) * P], w2_scales, z_words, z_scales, slice(0, S), f"bank{t}", False)
        out_rows = out.rearrange("(p t) s -> t p s", t=PACK)
        for t in range(PACK):
            above = sbuf([P, S], F32, f"above{t}")
            below = sbuf([P, S], F32, f"below{t}")
            res = sbuf([P, S], F32, f"res{t}")
            nc.scalar.activation(above[:], windows[t][:].indirect(n4_list[:]), ACT.Copy)
            nc.vector.tensor_tensor(above[:], above[:], windows[t][:, :S], ALU.subtract)
            nc.vector.tensor_scalar(above[:], above[:], 0.0, 0.5, ALU.max, ALU.mult)
            for cols in halves if t == PACK - 1 else (slice(0, S),):
                offsets = n3_list[:, cols.start // 16 : cols.stop // 16]
                nc.scalar.activation(below[:, cols], windows[t][:].indirect(offsets), ACT.Copy)
                nc.vector.tensor_tensor(below[:, cols], windows[t][:, cols], below[:, cols], ALU.subtract)
                nc.vector.scalar_tensor_tensor(res[:, cols], below[:, cols], 0.0, above[:, cols], ALU.max, ALU.add)
                nc.sync.dma_start(out_rows[t][:, cols], res[:, cols])
